import numpy as np
import ml_dtypes


def mxq(x, axis, fmt="e4m3"):
    dtype, down = {"e4m3": (ml_dtypes.float8_e4m3fn, 7), "e5m2": (ml_dtypes.float8_e5m2, 14)}[fmt]
    v = np.moveaxis(np.asarray(x, np.float32).astype(ml_dtypes.bfloat16).astype(np.float64), axis, -1)
    blocks = v.reshape(v.shape[:-1] + (-1, 32))
    amax = np.abs(blocks).max(-1, keepdims=True)
    byte = np.maximum(np.where(amax > 0, np.frexp(amax)[1] - 1 + 127, 0) - down, 1)
    scale = np.exp2(byte - 127.0)
    codes = (blocks / scale).astype(np.float32).astype(dtype).astype(np.float64)
    return np.moveaxis((codes * scale).reshape(v.shape), -1, axis)


WIDE = False


def mx_kscale(k):
    if not WIDE:
        return np.ones(k)
    levels = np.array([10, -10, 5, -5, 0])
    if k % 512:
        return np.exp2(np.random.permutation(np.resize(levels, k // 32))).repeat(32)
    a = np.empty((k // 512, 16))
    for p in range(k // 512):
        a[p, :8] = np.random.permutation(np.resize(levels, 8))
        for g in range(8):
            far = levels[np.abs(levels - a[p, g]) >= 10]
            a[p, g + 8] = far[np.random.randint(len(far))]
    return np.exp2(a.ravel()).repeat(32)


def f64(x):
    return np.asarray(x).astype(np.float64)


def striped(idx):
    return np.tile(idx.reshape(-1, 16).T, (8, 1)).astype(np.uint16)


def unstriped(offs):
    return offs[:16].T.reshape(-1).astype(np.int64)


def pack_weight(w):
    k, n = w.shape
    w = f64(np.asarray(w, np.float32).astype(ml_dtypes.bfloat16)).reshape(k // 32, 32, n)
    amax = np.abs(w).max(1)
    byte = np.clip(np.where(amax > 0, np.frexp(amax)[1] - 1 + 127 - 7, 1), 1, 254)
    scaled = (w * np.exp2(127.0 - byte)[:, None, :]).reshape(k, n).astype(np.float32)
    words = np.ascontiguousarray(scaled.reshape(k // 512, 128, 4, n).transpose(0, 1, 3, 2)).astype(ml_dtypes.float8_e4m3fn).view(np.uint8)
    return words, np.ascontiguousarray(byte.astype(np.uint8).reshape(k // 512, 16, n))


def unpack_weight(words, scales):
    g, p, n, _ = words.shape
    vals = np.ascontiguousarray(words).view(ml_dtypes.float8_e4m3fn).astype(np.float64) * np.repeat(np.exp2(scales.astype(np.float64) - 127.0), 8, axis=1)[..., None]
    return vals.transpose(0, 1, 3, 2).reshape(g * 512, n)


def relu(v):
    return np.maximum(v, 0.0)


K, T, S, D, N = 512, 1024, 512, 2, 128


def setup_inputs():
    n = np.random.standard_normal
    s = mx_kscale(K)[:, None]
    packed_xT = pack_weight(n((K, T)) * s)
    packed_eT = pack_weight(n((K, T)) * s)
    return {
        "x_words": packed_xT[0],
        "x_scales": packed_xT[1],
        "e_words": packed_eT[0],
        "e_scales": packed_eT[1],
        "wr": (n((K, N)) / np.sqrt(2 * K) / s).astype(np.float32),
        "wi": (n((K, N)) / np.sqrt(2 * K) / s).astype(np.float32),
        "yr": (n((N, S))).astype(np.float32),
        "yi": (n((N, S))).astype(np.float32),
        "offs": striped(np.random.permutation(T)[:S]),
    }


def reference(x_words, x_scales, e_words, e_scales, wr, wi, yr, yi, offs):
    xq = unpack_weight(x_words, x_scales)[:, unstriped(offs)]
    wrq = mxq(f64(wr), 0, "e4m3")
    e_offs = unpack_weight(e_words, e_scales)[:, unstriped(offs)]
    wiq = mxq(f64(wi), 0, "e4m3")
    t0 = wiq.T @ e_offs
    hr = (wrq.T @ xq) - t0
    hi = wrq.T @ e_offs + wiq.T @ xq
    h2 = (hr) ** 2 + (hi) ** 2
    nn = h2.reshape(len(h2), -1, D).sum(axis=2) + 0.2
    hy = hr * f64(yr) + hi * f64(yi)
    z = (hy.reshape(len(hy), -1, D).sum(axis=2)) / nn
    return nn * (z + relu(z - 0.6) - relu(-1.0 * z - 0.6))

@@ -1,0 +1,160 @@
+import math
+from contextlib import ExitStack
+
+import concourse.mybir as mybir
+
+F32 = mybir.dt.float32
+BF16 = mybir.dt.bfloat16
+I32 = mybir.dt.int32
+U32 = mybir.dt.uint32
+U16 = mybir.dt.uint16
+U8 = mybir.dt.uint8
+FP8X4 = mybir.dt.float8_e4m3fn_x4
+ALU = mybir.AluOpType
+ACT = mybir.ActivationFunctionType
+
+P = 128
+K, T, S, D, N = 512, 1024, 512, 2, 128
+PACK = 4
+HALF = S // 2
+FLOPS = 4 * 2 * K * N * S
+
+
+def tile_picked_yqam_soft_p_kernel(
+    tc, x_words, x_scales, e_words, e_scales, wr, wi, yr, yi, offs, out
+):
+    nc = tc.nc
+    with ExitStack() as ctx:
+        keep = ctx.enter_context(tc.tile_pool(name="keep", bufs=1))
+        psum = ctx.enter_context(tc.psum_pool(name="psum", bufs=1))
+
+        offsets = keep.tile([P, S // 16], U16, name="offsets")
+        x_scale_table = keep.tile([P, T], U8, name="x_scale_table")
+        e_scale_table = keep.tile([P, T], U8, name="e_scale_table")
+        x_word_table = keep.tile([P, T], I32, name="x_word_table")
+        e_word_table = keep.tile([P, T], I32, name="e_word_table")
+        wr_raw = keep.tile([P, PACK, N], F32, name="wr_raw")
+        wi_raw = keep.tile([P, PACK, N], F32, name="wi_raw")
+        yr_sb = keep.tile([P, S], F32, name="yr_sb")
+        yi_sb = keep.tile([P, S], F32, name="yi_sb")
+
+        def load_scales(table, scales, eng):
+            for q in range(4):
+                eng.dma_start(
+                    out=table[32 * q : 32 * q + 4, :].bitcast(I32),
+                    in_=scales[0, 4 * q : 4 * q + 4, :].bitcast(I32),
+                )
+
+        def load_words(table, words):
+            nc.sync.dma_start(out=table[:], in_=words[0].rearrange("p n t -> p (n t)").bitcast(I32))
+
+        def load_weight(raw, w):
+            nc.sync.dma_start(out=raw[:], in_=w.rearrange("(p j) m -> p j m", j=PACK))
+
+        nc.vector.memset(x_scale_table[:].bitcast(I32), 0)
+        nc.vector.memset(e_scale_table[:].bitcast(I32), 0)
+        nc.sync.dma_start(offsets[:], offs)
+        load_scales(x_scale_table, x_scales, nc.sync)
+        load_words(x_word_table, x_words)
+        load_weight(wi_raw, wi)
+        load_weight(wr_raw, wr)
+        load_scales(e_scale_table, e_scales, nc.sync)
+        load_words(e_word_table, e_words)
+        nc.sync.dma_start(out=yi_sb[:], in_=yi)
+        nc.sync.dma_start(out=yr_sb[:], in_=yr)
+
+        def interleave(raw, sign, name):
+            grouped = keep.tile([P, N, PACK], BF16, name=name + "_grouped", align_bytes=64)
+            nc.scalar.activation(
+                out=grouped[:].rearrange("p (c i) t -> p c t i", i=4),
+                in_=raw[:].rearrange("p t (c i) -> p c t i", i=4),
+                func=ACT.Copy,
+                scale=sign,
+            )
+            return grouped
+
+        def quantize(grouped, name):
+            codes = keep.tile([P, N], U32, name=name + "_codes", align_bytes=64)
+            scales = keep.tile([P, N], U8, name=name + "_scales", align_bytes=64)
+            nc.vector.quantize_mx(
+                out=codes[:].bitcast(FP8X4),
+                scales=scales[:],
+                in_=grouped[:].rearrange("p m t -> p (m t)"),
+            )
+            return codes, scales
+
+        def gather(window, dtype, first, count, name):
+            picked = keep.tile([P, count], dtype, name=name, align_bytes=64)
+            nc.vector.tensor_copy(
+                out=picked[:], in_=window.indirect(offsets[:, first // 16 : (first + count) // 16])
+            )
+            return picked
+
+        wi_grouped = interleave(wi_raw, 1.0, "wi")
+        wr_grouped = interleave(wr_raw, 1.0, "wr")
+        wn_grouped = interleave(wi_raw, -1.0, "wn")
+
+        x_picked_scales = gather(x_scale_table[:], U8, 0, S, "x_picked_scales")
+        x_picked = gather(x_word_table[:].bitcast(U32), U32, 0, S, "x_picked")
+        e_all = gather(e_scale_table[:], U8, 0, S, "e_picked_scales")
+        e_picked_scales = [e_all[:, h * HALF : (h + 1) * HALF] for h in range(2)]
+        wi_q = quantize(wi_grouped, "wi")
+        wr_q = quantize(wr_grouped, "wr")
+        wn_q = quantize(wn_grouped, "wn")
+        e_picked = [gather(e_word_table[:].bitcast(U32), U32, h * HALF, HALF, f"e_picked{h}") for h in range(2)]
+
+        def mx(bank, weight, codes, scales, start):
+            nc.tensor.matmul_mx(
+                out=bank[:],
+                lhsT=weight[0][:].bitcast(FP8X4),
+                lhsT_scale=weight[1][:],
+                rhs=codes.bitcast(FP8X4),
+                rhs_scale=scales,
+                start=start,
+                stop=not start,
+            )
+
+        hr, hi = [], []
+        for h in range(2):
+            cols = slice(h * HALF, (h + 1) * HALF)
+            hr.append(psum.tile([P, HALF], F32, name=f"hr{h}"))
+            hi.append(psum.tile([P, HALF], F32, name=f"hi{h}"))
+            mx(hi[h], wi_q, x_picked[:, cols], x_picked_scales[:, cols], True)
+            mx(hr[h], wr_q, x_picked[:, cols], x_picked_scales[:, cols], True)
+            mx(hi[h], wr_q, e_picked[h][:], e_picked_scales[h], False)
+            mx(hr[h], wn_q, e_picked[h][:], e_picked_scales[h], False)
+
+        V = HALF // D
+        def tiles(name, width):
+            return [keep.tile([P, width], F32, name=f"{name}{h}") for h in range(2)]
+
+        sq_r, sq_i, p_r, p_i = tiles("sq_r", HALF), tiles("sq_i", HALF), tiles("p_r", HALF), tiles("p_i", HALF)
+        h2, hy = tiles("h2", HALF), tiles("hy", HALF)
+        s, c, low, clip, res = tiles("s", V), tiles("c", V), tiles("low", V), tiles("clip", V), tiles("res", V)
+        root = math.sqrt(0.6)
+        for h in range(2):
+            cols = slice(h * HALF, (h + 1) * HALF)
+            nc.scalar.activation(out=sq_i[h][:], in_=hi[h][:], func=ACT.Square, scale=root)
+            nc.scalar.activation(out=sq_r[h][:], in_=hr[h][:], func=ACT.Square, scale=root)
+            nc.vector.tensor_tensor(out=p_i[h][:], in0=hi[h][:], in1=yi_sb[:, cols], op=ALU.mult)
+            nc.vector.tensor_tensor(out=p_r[h][:], in0=hr[h][:], in1=yr_sb[:, cols], op=ALU.mult)
+            nc.vector.tensor_tensor(out=h2[h][:], in0=sq_r[h][:], in1=sq_i[h][:], op=ALU.add)
+        for h in range(2):
+            nc.vector.tensor_tensor(out=hy[h][:], in0=p_r[h][:], in1=p_i[h][:], op=ALU.add)
+        for h in range(2):
+            nc.vector.scalar_tensor_tensor(
+                out=c[h][:], in0=h2[h][:, 0::2], scalar=0.6 * 0.2, in1=h2[h][:, 1::2], op0=ALU.add, op1=ALU.add
+            )
+        for h in range(2):
+            nc.vector.tensor_tensor(out=s[h][:], in0=hy[h][:, 0::2], in1=hy[h][:, 1::2], op=ALU.add)
+        for h in range(2):
+            nc.vector.tensor_tensor(out=low[h][:], in0=s[h][:], in1=c[h][:], op=ALU.min)
+        for h in range(2):
+            nc.vector.scalar_tensor_tensor(
+                out=clip[h][:], in0=c[h][:], scalar=-1.0, in1=low[h][:], op0=ALU.mult, op1=ALU.max
+            )
+        for h in range(2):
+            nc.vector.scalar_tensor_tensor(
+                out=res[h][:], in0=s[h][:], scalar=2.0, in1=clip[h][:], op0=ALU.mult, op1=ALU.subtract
+            )
+            nc.sync.dma_start(out=out[:, h * V : (h + 1) * V], in_=res[h][:])

@@ -2,6 +2,7 @@ import math
 from contextlib import ExitStack
 
 import concourse.mybir as mybir
+from concourse.masks import make_identity
 
 F32 = mybir.dt.float32
 BF16 = mybir.dt.bfloat16
@@ -40,7 +41,7 @@ def tile_picked_yqam_soft_p_kernel(
 
         def load_scales(table, scales, eng):
             for q in range(4):
-                eng.dma_start(
+                eng[q].dma_start(
                     out=table[32 * q : 32 * q + 4, :].bitcast(I32),
                     in_=scales[0, 4 * q : 4 * q + 4, :].bitcast(I32),
                 )
@@ -53,12 +54,14 @@ def tile_picked_yqam_soft_p_kernel(
 
         nc.vector.memset(x_scale_table[:].bitcast(I32), 0)
         nc.vector.memset(e_scale_table[:].bitcast(I32), 0)
+        identity = keep.tile([P, P], F32, name="identity")
+        make_identity(nc, identity[:])
         nc.sync.dma_start(offsets[:], offs)
-        load_scales(x_scale_table, x_scales, nc.sync)
+        load_scales(x_scale_table, x_scales, (nc.sync, nc.scalar, nc.sync, nc.scalar))
         load_words(x_word_table, x_words)
         load_weight(wi_raw, wi)
         load_weight(wr_raw, wr)
-        load_scales(e_scale_table, e_scales, nc.sync)
+        load_scales(e_scale_table, e_scales, (nc.sync,) * 4)
         load_words(e_word_table, e_words)
         nc.sync.dma_start(out=yi_sb[:], in_=yi)
         nc.sync.dma_start(out=yr_sb[:], in_=yr)
@@ -91,8 +94,8 @@ def tile_picked_yqam_soft_p_kernel(
             return picked
 
         wi_grouped = interleave(wi_raw, 1.0, "wi")
-        wr_grouped = interleave(wr_raw, 1.0, "wr")
         wn_grouped = interleave(wi_raw, -1.0, "wn")
+        wr_grouped = interleave(wr_raw, 1.0, "wr")
 
         x_picked_scales = gather(x_scale_table[:], U8, 0, S, "x_picked_scales")
         x_picked = gather(x_word_table[:].bitcast(U32), U32, 0, S, "x_picked")
@@ -125,36 +128,66 @@ def tile_picked_yqam_soft_p_kernel(
             mx(hr[h], wn_q, e_picked[h][:], e_picked_scales[h], False)
 
         V = HALF // D
-        def tiles(name, width):
-            return [keep.tile([P, width], F32, name=f"{name}{h}") for h in range(2)]
+        def tiles(name, *shape):
+            return [keep.tile([P, *shape], F32, name=f"{name}{h}") for h in range(2)]
 
-        sq_r, sq_i, p_r, p_i = tiles("sq_r", HALF), tiles("sq_i", HALF), tiles("p_r", HALF), tiles("p_i", HALF)
-        h2, hy = tiles("h2", HALF), tiles("hy", HALF)
-        s, c, low, clip, res = tiles("s", V), tiles("c", V), tiles("low", V), tiles("clip", V), tiles("res", V)
+        def dealt(ap):
+            return ap.rearrange("p (v d) -> p d v", d=D)
+
+        def turned_sum(bank, first, second):
+            terms = [tile[:, d, :] for tile in (first, second) for d in range(D)]
+            for n, term in enumerate(terms):
+                nc.tensor.matmul(
+                    bank[:], term, identity[:], is_transpose=True, start=(n == 0), stop=(n == len(terms) - 1)
+                )
+
+        sq_r, sq_i, p_r, p_i = tiles("sq_r", D, V), tiles("sq_i", D, V), tiles("p_r", D, V), tiles("p_i", D, V)
+        hy = keep.tile([P, D, V], F32, name="hy")
+        low, clip, res, c = tiles("low", V), tiles("clip", V), tiles("res", V), tiles("c", V)
+        c_sum = psum.tile([P, N], F32, name="c_sum")
+        c_imag = keep.tile([P, V], F32, name="c_imag")
+        c_real = keep.tile([P, V], F32, name="c_real")
+        s = [psum.tile([P, N], F32, name="s0"), keep.tile([P, V], F32, name="s1")]
+        res_back = psum.tile([P, V], F32, name="res_back")
+        res_out = keep.tile([P, V], F32, name="res_out")
         root = math.sqrt(0.6)
         for h in range(2):
             cols = slice(h * HALF, (h + 1) * HALF)
-            nc.scalar.activation(out=sq_i[h][:], in_=hi[h][:], func=ACT.Square, scale=root)
-            nc.scalar.activation(out=sq_r[h][:], in_=hr[h][:], func=ACT.Square, scale=root)
-            nc.vector.tensor_tensor(out=p_i[h][:], in0=hi[h][:], in1=yi_sb[:, cols], op=ALU.mult)
-            nc.vector.tensor_tensor(out=p_r[h][:], in0=hr[h][:], in1=yr_sb[:, cols], op=ALU.mult)
-            nc.vector.tensor_tensor(out=h2[h][:], in0=sq_r[h][:], in1=sq_i[h][:], op=ALU.add)
-        for h in range(2):
-            nc.vector.tensor_tensor(out=hy[h][:], in0=p_r[h][:], in1=p_i[h][:], op=ALU.add)
-        for h in range(2):
-            nc.vector.scalar_tensor_tensor(
-                out=c[h][:], in0=h2[h][:, 0::2], scalar=0.6 * 0.2, in1=h2[h][:, 1::2], op0=ALU.add, op1=ALU.add
-            )
-        for h in range(2):
-            nc.vector.tensor_tensor(out=s[h][:], in0=hy[h][:, 0::2], in1=hy[h][:, 1::2], op=ALU.add)
-        for h in range(2):
-            nc.vector.tensor_tensor(out=low[h][:], in0=s[h][:], in1=c[h][:], op=ALU.min)
-        for h in range(2):
+            nc.scalar.activation(out=sq_i[h][:], in_=dealt(hi[h][:]), func=ACT.Square, scale=root)
+            nc.scalar.activation(out=sq_r[h][:], in_=dealt(hr[h][:]), func=ACT.Square, scale=root)
+            nc.vector.tensor_tensor(out=p_i[h][:], in0=dealt(hi[h][:]), in1=dealt(yi_sb[:, cols]), op=ALU.mult)
+            nc.vector.tensor_tensor(out=p_r[h][:], in0=dealt(hr[h][:]), in1=dealt(yr_sb[:, cols]), op=ALU.mult)
+        turned_sum(c_sum, sq_i[0], sq_r[0])
+        turned_sum(s[0], p_i[0], p_r[0])
+        nc.scalar.activation(out=c[0][:], in_=c_sum[:], func=ACT.Copy, bias=0.6 * 0.2)
+        nc.vector.scalar_tensor_tensor(
+            out=c_imag[:], in0=sq_i[1][:, 0, :], scalar=0.6 * 0.2, in1=sq_i[1][:, 1, :], op0=ALU.add, op1=ALU.add
+        )
+        nc.vector.tensor_tensor(out=c_real[:], in0=sq_r[1][:, 0, :], in1=sq_r[1][:, 1, :], op=ALU.add)
+
+        def step_low(h):
+            nc.vector.tensor_tensor(out=low[h][:], in0=c[h][:], in1=s[h][:], op=ALU.min)
+
+        def step_clip(h):
             nc.vector.scalar_tensor_tensor(
                 out=clip[h][:], in0=c[h][:], scalar=-1.0, in1=low[h][:], op0=ALU.mult, op1=ALU.max
             )
-        for h in range(2):
+
+        def step_res(h):
             nc.vector.scalar_tensor_tensor(
                 out=res[h][:], in0=s[h][:], scalar=2.0, in1=clip[h][:], op0=ALU.mult, op1=ALU.subtract
             )
-            nc.sync.dma_start(out=out[:, h * V : (h + 1) * V], in_=res[h][:])
+
+        step_low(0)
+        nc.vector.tensor_tensor(out=hy[:], in0=p_r[1][:], in1=p_i[1][:], op=ALU.add)
+        step_clip(0)
+        nc.vector.tensor_tensor(out=c[1][:], in0=c_imag[:], in1=c_real[:], op=ALU.add)
+        nc.vector.tensor_tensor(out=s[1][:], in0=hy[:, 0, :], in1=hy[:, 1, :], op=ALU.add)
+        step_res(0)
+        nc.tensor.transpose(res_back[:], res[0][:], identity[:])
+        nc.scalar.copy(out=res_out[:], in_=res_back[:])
+        nc.sync.dma_start(out=out[:, 0:V], in_=res_out[:])
+        step_low(1)
+        step_clip(1)
+        step_res(1)
+        nc.sync.dma_start(out=out[:, V : 2 * V], in_=res[1][:])

@@ -60,31 +60,29 @@ def tile_picked_yqam_soft_p_kernel(
         load_scales(x_scale_table, x_scales, (nc.sync, nc.scalar, nc.sync, nc.scalar))
         load_words(x_word_table, x_words)
         load_weight(wi_raw, wi)
-        load_weight(wr_raw, wr)
         load_scales(e_scale_table, e_scales, (nc.sync,) * 4)
+        load_weight(wr_raw, wr)
         load_words(e_word_table, e_words)
         nc.sync.dma_start(out=yi_sb[:], in_=yi)
         nc.sync.dma_start(out=yr_sb[:], in_=yr)
 
-        def interleave(raw, sign, name):
-            grouped = keep.tile([P, N, PACK], BF16, name=name + "_grouped", align_bytes=64)
+        def interleave(grouped, raw, sign):
             nc.scalar.activation(
-                out=grouped[:].rearrange("p (c i) t -> p c t i", i=4),
+                out=grouped.rearrange("p (c i) t -> p c t i", i=4),
                 in_=raw[:].rearrange("p t (c i) -> p c t i", i=4),
                 func=ACT.Copy,
                 scale=sign,
             )
-            return grouped
 
-        def quantize(grouped, name):
-            codes = keep.tile([P, N], U32, name=name + "_codes", align_bytes=64)
-            scales = keep.tile([P, N], U8, name=name + "_scales", align_bytes=64)
+        def quantize(grouped, count, name, codes_tag):
+            codes = keep.tile([P, count * N], U32, name=name + "_codes", tag=codes_tag, align_bytes=64)
+            scales = keep.tile([P, count * N], U8, name=name + "_scales", align_bytes=64)
             nc.vector.quantize_mx(
                 out=codes[:].bitcast(FP8X4),
                 scales=scales[:],
-                in_=grouped[:].rearrange("p m t -> p (m t)"),
+                in_=grouped[:].rearrange("p w m t -> p (w m t)"),
             )
-            return codes, scales
+            return [(codes[:, w * N : (w + 1) * N], scales[:, w * N : (w + 1) * N]) for w in range(count)]
 
         def gather(window, dtype, first, count, name):
             picked = keep.tile([P, count], dtype, name=name, align_bytes=64)
@@ -93,24 +91,25 @@ def tile_picked_yqam_soft_p_kernel(
             )
             return picked
 
-        wi_grouped = interleave(wi_raw, 1.0, "wi")
-        wn_grouped = interleave(wi_raw, -1.0, "wn")
-        wr_grouped = interleave(wr_raw, 1.0, "wr")
+        early_grouped = keep.tile([P, 1, N, PACK], BF16, name="early_grouped", align_bytes=64)
+        late_grouped = keep.tile([P, 2, N, PACK], BF16, name="late_grouped", align_bytes=64)
+        interleave(early_grouped[:, 0], wi_raw, 1.0)
+        interleave(late_grouped[:, 0], wi_raw, -1.0)
+        interleave(late_grouped[:, 1], wr_raw, 1.0)
 
         x_picked_scales = gather(x_scale_table[:], U8, 0, S, "x_picked_scales")
         x_picked = gather(x_word_table[:].bitcast(U32), U32, 0, S, "x_picked")
         e_all = gather(e_scale_table[:], U8, 0, S, "e_picked_scales")
         e_picked_scales = [e_all[:, h * HALF : (h + 1) * HALF] for h in range(2)]
-        wi_q = quantize(wi_grouped, "wi")
-        wr_q = quantize(wr_grouped, "wr")
-        wn_q = quantize(wn_grouped, "wn")
+        (wi_q,) = quantize(early_grouped, 1, "early", "early_codes")
+        wn_q, wr_q = quantize(late_grouped, 2, "late", "late_codes")
         e_picked = [gather(e_word_table[:].bitcast(U32), U32, h * HALF, HALF, f"e_picked{h}") for h in range(2)]
 
         def mx(bank, weight, codes, scales, start):
             nc.tensor.matmul_mx(
                 out=bank[:],
-                lhsT=weight[0][:].bitcast(FP8X4),
-                lhsT_scale=weight[1][:],
+                lhsT=weight[0].bitcast(FP8X4),
+                lhsT_scale=weight[1],
                 rhs=codes.bitcast(FP8X4),
                 rhs_scale=scales,
                 start=start,

@@ -144,11 +144,13 @@ def tile_picked_yqam_soft_p_kernel(
         hy = keep.tile([P, D, V], F32, name="hy")
         low, clip, res, c = tiles("low", V), tiles("clip", V), tiles("res", V), tiles("c", V)
         c_sum = psum.tile([P, N], F32, name="c_sum")
+        s_sum = psum.tile([P, N], F32, name="s_sum")
+        c_back = psum.tile([P, V], F32, name="c_back")
+        c_turned = keep.tile([P, N], F32, name="c_turned")
+        s_turned = keep.tile([P, N], F32, name="s_turned")
         c_imag = keep.tile([P, V], F32, name="c_imag")
         c_real = keep.tile([P, V], F32, name="c_real")
-        s = [psum.tile([P, N], F32, name="s0"), keep.tile([P, V], F32, name="s1")]
-        res_back = psum.tile([P, V], F32, name="res_back")
-        res_out = keep.tile([P, V], F32, name="res_out")
+        s = [psum.tile([P, V], F32, name="s0"), keep.tile([P, V], F32, name="s1")]
         root = math.sqrt(0.6)
         for h in range(2):
             cols = slice(h * HALF, (h + 1) * HALF)
@@ -157,36 +159,27 @@ def tile_picked_yqam_soft_p_kernel(
             nc.vector.tensor_tensor(out=p_i[h][:], in0=dealt(hi[h][:]), in1=dealt(yi_sb[:, cols]), op=ALU.mult)
             nc.vector.tensor_tensor(out=p_r[h][:], in0=dealt(hr[h][:]), in1=dealt(yr_sb[:, cols]), op=ALU.mult)
         turned_sum(c_sum, sq_i[0], sq_r[0])
-        turned_sum(s[0], p_i[0], p_r[0])
-        nc.scalar.activation(out=c[0][:], in_=c_sum[:], func=ACT.Copy, bias=0.6 * 0.2)
+        turned_sum(s_sum, p_i[0], p_r[0])
+        nc.scalar.copy(out=c_turned[:], in_=c_sum[:])
+        nc.tensor.transpose(c_back[:], c_turned[:], identity[:])
+        nc.scalar.copy(out=s_turned[:], in_=s_sum[:])
+        nc.tensor.transpose(s[0][:], s_turned[:], identity[:])
+        nc.scalar.activation(out=c[0][:], in_=c_back[:], func=ACT.Copy, bias=0.6 * 0.2)
         nc.vector.scalar_tensor_tensor(
             out=c_imag[:], in0=sq_i[1][:, 0, :], scalar=0.6 * 0.2, in1=sq_i[1][:, 1, :], op0=ALU.add, op1=ALU.add
         )
         nc.vector.tensor_tensor(out=c_real[:], in0=sq_r[1][:, 0, :], in1=sq_r[1][:, 1, :], op=ALU.add)
-
-        def step_low(h):
-            nc.vector.tensor_tensor(out=low[h][:], in0=c[h][:], in1=s[h][:], op=ALU.min)
-
-        def step_clip(h):
+        nc.vector.tensor_tensor(out=hy[:], in0=p_r[1][:], in1=p_i[1][:], op=ALU.add)
+        nc.vector.tensor_tensor(out=c[1][:], in0=c_imag[:], in1=c_real[:], op=ALU.add)
+        nc.vector.tensor_tensor(out=s[1][:], in0=hy[:, 0, :], in1=hy[:, 1, :], op=ALU.add)
+        for h in range(2):
+            nc.vector.tensor_tensor(out=low[h][:], in0=s[h][:], in1=c[h][:], op=ALU.min)
+        for h in range(2):
             nc.vector.scalar_tensor_tensor(
                 out=clip[h][:], in0=c[h][:], scalar=-1.0, in1=low[h][:], op0=ALU.mult, op1=ALU.max
             )
-
-        def step_res(h):
+        for h in range(2):
             nc.vector.scalar_tensor_tensor(
                 out=res[h][:], in0=s[h][:], scalar=2.0, in1=clip[h][:], op0=ALU.mult, op1=ALU.subtract
             )
-
-        step_low(0)
-        nc.vector.tensor_tensor(out=hy[:], in0=p_r[1][:], in1=p_i[1][:], op=ALU.add)
-        step_clip(0)
-        nc.vector.tensor_tensor(out=c[1][:], in0=c_imag[:], in1=c_real[:], op=ALU.add)
-        nc.vector.tensor_tensor(out=s[1][:], in0=hy[:, 0, :], in1=hy[:, 1, :], op=ALU.add)
-        step_res(0)
-        nc.tensor.transpose(res_back[:], res[0][:], identity[:])
-        nc.scalar.copy(out=res_out[:], in_=res_back[:])
-        nc.sync.dma_start(out=out[:, 0:V], in_=res_out[:])
-        step_low(1)
-        step_clip(1)
-        step_res(1)
-        nc.sync.dma_start(out=out[:, V : 2 * V], in_=res[1][:])
+            nc.sync.dma_start(out=out[:, h * V : (h + 1) * V], in_=res[h][:])

import math
from contextlib import ExitStack

import concourse.mybir as mybir
from concourse.masks import make_identity

F32 = mybir.dt.float32
BF16 = mybir.dt.bfloat16
I32 = mybir.dt.int32
U32 = mybir.dt.uint32
U16 = mybir.dt.uint16
U8 = mybir.dt.uint8
FP8X4 = mybir.dt.float8_e4m3fn_x4
ALU = mybir.AluOpType
ACT = mybir.ActivationFunctionType

P = 128
K, T, S, D, N = 512, 1024, 512, 2, 128
PACK = 4
HALF = S // 2
FLOPS = 4 * 2 * K * N * S


def tile_picked_yqam_soft_p_kernel(
    tc, x_words, x_scales, e_words, e_scales, wr, wi, yr, yi, offs, out
):
    nc = tc.nc
    with ExitStack() as ctx:
        keep = ctx.enter_context(tc.tile_pool(name="keep", bufs=1))
        psum = ctx.enter_context(tc.psum_pool(name="psum", bufs=1))

        offsets = keep.tile([P, S // 16], U16, name="offsets")
        x_scale_table = keep.tile([P, T], U8, name="x_scale_table")
        e_scale_table = keep.tile([P, T], U8, name="e_scale_table")
        x_word_table = keep.tile([P, T], I32, name="x_word_table")
        e_word_table = keep.tile([P, T], I32, name="e_word_table")
        wr_raw = keep.tile([P, PACK, N], F32, name="wr_raw")
        wi_raw = keep.tile([P, PACK, N], F32, name="wi_raw")
        yr_sb = keep.tile([P, S], F32, name="yr_sb")
        yi_sb = keep.tile([P, S], F32, name="yi_sb")

        def load_scales(table, scales, eng):
            for q in range(4):
                eng[q].dma_start(
                    out=table[32 * q : 32 * q + 4, :].bitcast(I32),
                    in_=scales[0, 4 * q : 4 * q + 4, :].bitcast(I32),
                )

        def load_words(table, words):
            nc.sync.dma_start(out=table[:], in_=words[0].rearrange("p n t -> p (n t)").bitcast(I32))

        def load_weight(raw, w):
            nc.sync.dma_start(out=raw[:], in_=w.rearrange("(p j) m -> p j m", j=PACK))

        nc.vector.memset(x_scale_table[:].bitcast(I32), 0)
        nc.vector.memset(e_scale_table[:].bitcast(I32), 0)
        identity = keep.tile([P, P], F32, name="identity")
        make_identity(nc, identity[:])
        nc.sync.dma_start(offsets[:], offs)
        load_scales(x_scale_table, x_scales, (nc.sync, nc.scalar, nc.sync, nc.scalar))
        load_words(x_word_table, x_words)
        load_weight(wi_raw, wi)
        load_scales(e_scale_table, e_scales, (nc.sync,) * 4)
        load_weight(wr_raw, wr)
        load_words(e_word_table, e_words)
        nc.sync.dma_start(out=yi_sb[:], in_=yi)
        nc.sync.dma_start(out=yr_sb[:], in_=yr)

        def interleave(grouped, raw, sign):
            nc.scalar.activation(
                out=grouped.rearrange("p (c i) t -> p c t i", i=4),
                in_=raw[:].rearrange("p t (c i) -> p c t i", i=4),
                func=ACT.Copy,
                scale=sign,
            )

        def quantize(grouped, count, name, codes_tag):
            codes = keep.tile([P, count * N], U32, name=name + "_codes", tag=codes_tag, align_bytes=64)
            scales = keep.tile([P, count * N], U8, name=name + "_scales", align_bytes=64)
            nc.vector.quantize_mx(
                out=codes[:].bitcast(FP8X4),
                scales=scales[:],
                in_=grouped[:].rearrange("p w m t -> p (w m t)"),
            )
            return [(codes[:, w * N : (w + 1) * N], scales[:, w * N : (w + 1) * N]) for w in range(count)]

        def gather(window, dtype, first, count, name):
            picked = keep.tile([P, count], dtype, name=name, align_bytes=64)
            nc.vector.tensor_copy(
                out=picked[:], in_=window.indirect(offsets[:, first // 16 : (first + count) // 16])
            )
            return picked

        early_grouped = keep.tile([P, 1, N, PACK], BF16, name="early_grouped", align_bytes=64)
        late_grouped = keep.tile([P, 2, N, PACK], BF16, name="late_grouped", align_bytes=64)
        interleave(early_grouped[:, 0], wi_raw, 1.0)
        interleave(late_grouped[:, 0], wi_raw, -1.0)
        interleave(late_grouped[:, 1], wr_raw, 1.0)

        x_picked_scales = gather(x_scale_table[:], U8, 0, S, "x_picked_scales")
        x_picked = gather(x_word_table[:].bitcast(U32), U32, 0, S, "x_picked")
        e_all = gather(e_scale_table[:], U8, 0, S, "e_picked_scales")
        e_picked_scales = [e_all[:, h * HALF : (h + 1) * HALF] for h in range(2)]
        (wi_q,) = quantize(early_grouped, 1, "early", "early_codes")
        wn_q, wr_q = quantize(late_grouped, 2, "late", "late_codes")
        e_picked = [gather(e_word_table[:].bitcast(U32), U32, h * HALF, HALF, f"e_picked{h}") for h in range(2)]

        def mx(bank, weight, codes, scales, start):
            nc.tensor.matmul_mx(
                out=bank[:],
                lhsT=weight[0].bitcast(FP8X4),
                lhsT_scale=weight[1],
                rhs=codes.bitcast(FP8X4),
                rhs_scale=scales,
                start=start,
                stop=not start,
            )

        hr, hi = [], []
        for h in range(2):
            cols = slice(h * HALF, (h + 1) * HALF)
            hr.append(psum.tile([P, HALF], F32, name=f"hr{h}"))
            hi.append(psum.tile([P, HALF], F32, name=f"hi{h}"))
            mx(hi[h], wi_q, x_picked[:, cols], x_picked_scales[:, cols], True)
            mx(hr[h], wr_q, x_picked[:, cols], x_picked_scales[:, cols], True)
            mx(hi[h], wr_q, e_picked[h][:], e_picked_scales[h], False)
            mx(hr[h], wn_q, e_picked[h][:], e_picked_scales[h], False)

        V = HALF // D
        def tiles(name, *shape):
            return [keep.tile([P, *shape], F32, name=f"{name}{h}") for h in range(2)]

        def dealt(ap):
            return ap.rearrange("p (v d) -> p d v", d=D)

        def turned_sum(bank, first, second):
            terms = [tile[:, d, :] for tile in (first, second) for d in range(D)]
            for n, term in enumerate(terms):
                nc.tensor.matmul(
                    bank[:], term, identity[:], is_transpose=True, start=(n == 0), stop=(n == len(terms) - 1)
                )

        sq_r, sq_i, p_r, p_i = tiles("sq_r", D, V), tiles("sq_i", D, V), tiles("p_r", D, V), tiles("p_i", D, V)
        hy = keep.tile([P, D, V], F32, name="hy")
        low, clip, res, c = tiles("low", V), tiles("clip", V), tiles("res", V), tiles("c", V)
        c_sum = psum.tile([P, N], F32, name="c_sum")
        s_sum = psum.tile([P, N], F32, name="s_sum")
        c_back = psum.tile([P, V], F32, name="c_back")
        c_turned = keep.tile([P, N], F32, name="c_turned")
        s_turned = keep.tile([P, N], F32, name="s_turned")
        c_imag = keep.tile([P, V], F32, name="c_imag")
        c_real = keep.tile([P, V], F32, name="c_real")
        s = [psum.tile([P, V], F32, name="s0"), keep.tile([P, V], F32, name="s1")]
        root = math.sqrt(0.6)
        for h in range(2):
            cols = slice(h * HALF, (h + 1) * HALF)
            nc.scalar.activation(out=sq_i[h][:], in_=dealt(hi[h][:]), func=ACT.Square, scale=root)
            nc.scalar.activation(out=sq_r[h][:], in_=dealt(hr[h][:]), func=ACT.Square, scale=root)
            nc.vector.tensor_tensor(out=p_i[h][:], in0=dealt(hi[h][:]), in1=dealt(yi_sb[:, cols]), op=ALU.mult)
            nc.vector.tensor_tensor(out=p_r[h][:], in0=dealt(hr[h][:]), in1=dealt(yr_sb[:, cols]), op=ALU.mult)
        turned_sum(c_sum, sq_i[0], sq_r[0])
        turned_sum(s_sum, p_i[0], p_r[0])
        nc.scalar.copy(out=c_turned[:], in_=c_sum[:])
        nc.tensor.transpose(c_back[:], c_turned[:], identity[:])
        nc.scalar.copy(out=s_turned[:], in_=s_sum[:])
        nc.tensor.transpose(s[0][:], s_turned[:], identity[:])
        nc.scalar.activation(out=c[0][:], in_=c_back[:], func=ACT.Copy, bias=0.6 * 0.2)
        nc.vector.scalar_tensor_tensor(
            out=c_imag[:], in0=sq_i[1][:, 0, :], scalar=0.6 * 0.2, in1=sq_i[1][:, 1, :], op0=ALU.add, op1=ALU.add
        )
        nc.vector.tensor_tensor(out=c_real[:], in0=sq_r[1][:, 0, :], in1=sq_r[1][:, 1, :], op=ALU.add)
        nc.vector.tensor_tensor(out=hy[:], in0=p_r[1][:], in1=p_i[1][:], op=ALU.add)
        nc.vector.tensor_tensor(out=c[1][:], in0=c_imag[:], in1=c_real[:], op=ALU.add)
        nc.vector.tensor_tensor(out=s[1][:], in0=hy[:, 0, :], in1=hy[:, 1, :], op=ALU.add)
        for h in range(2):
            nc.vector.tensor_tensor(out=low[h][:], in0=s[h][:], in1=c[h][:], op=ALU.min)
        for h in range(2):
            nc.vector.scalar_tensor_tensor(
                out=clip[h][:], in0=c[h][:], scalar=-1.0, in1=low[h][:], op0=ALU.mult, op1=ALU.max
            )
        for h in range(2):
            nc.vector.scalar_tensor_tensor(
                out=res[h][:], in0=s[h][:], scalar=2.0, in1=clip[h][:], op0=ALU.mult, op1=ALU.subtract
            )
            nc.sync.dma_start(out=out[:, h * V : (h + 1) * V], in_=res[h][:])
